import numpy as np
import ml_dtypes

BF16 = ml_dtypes.bfloat16


def bf(x):
    return np.asarray(x, np.float32).astype(BF16)


def f32(x):
    return np.asarray(x, np.float32)


def f64(x):
    return np.asarray(x).astype(np.float64)


def striped(idx):
    return np.tile(idx.reshape(-1, 16).T, (8, 1))


S, K, M, N, D, V = 512, 128, 256, 256, 2, 128


def setup_inputs():
    return {"table": bf(np.random.standard_normal((S, K))), "w": bf(np.random.standard_normal((D, K, M)) / np.sqrt(D * K)), "b": f32(0.5 * np.random.standard_normal((M, 1))), "offs": striped(np.random.permutation(S)[:N])}


def reference(table, w, b, offs):
    idx = offs[:16].T.reshape(-1)
    x = f64(table)[idx].T
    y = sum(f64(w)[t].T @ x[:, t * V : (t + 1) * V] for t in range(D))
    return np.maximum(y + f64(b), 0.0)

@@ -1,0 +1,75 @@
+import concourse.mybir as mybir
+from concourse.masks import make_identity
+
+BF16, F32, U16 = mybir.dt.bfloat16, mybir.dt.float32, mybir.dt.uint16
+
+P = 128
+NODES = 512
+ENDS = 2
+EDGES = 128
+OUT_FEATURES = 256
+NODE_BLOCKS = NODES // P
+OUT_BLOCKS = OUT_FEATURES // P
+COLS_PER_END = EDGES // 16
+
+FLOPS = 2 * ENDS * P * OUT_FEATURES * EDGES
+
+
+def tile_gather_matmul_kernel(tc, table, w, b, offs, out):
+    nc = tc.nc
+    with (
+        tc.tile_pool(name="held", bufs=1) as held,
+        tc.psum_pool(name="psum", bufs=1) as psum,
+    ):
+        offsets = held.tile([P, ENDS * COLS_PER_END], U16, name="offsets")
+        nc.sync.dma_start(offsets[:], offs)
+
+        node_rows = [held.tile([P, P], BF16, name=f"node_rows{i}") for i in range(NODE_BLOCKS)]
+        for i in range(NODE_BLOCKS):
+            queue = nc.sync if i % 2 == 0 else nc.scalar
+            queue.dma_start(node_rows[i][:], table[i * P : (i + 1) * P, :])
+
+        weights = held.tile([P, ENDS, OUT_FEATURES], BF16, name="weights")
+        nc.sync.dma_start(weights[:], w.rearrange("t k m -> k t m"))
+        bias = held.tile([P, OUT_BLOCKS], F32, name="bias")
+        with nc.allow_non_contiguous_dma(reason="256 single float32 values, one to a partition and column"):
+            nc.scalar.dma_start(bias[:], b.rearrange("(j p) o -> p (j o)", p=P))
+
+        identity = held.tile([P, P], BF16, name="identity")
+        make_identity(nc, identity[:])
+
+        node_columns = held.tile([P, NODES], BF16, name="node_columns")
+        for i in range(NODE_BLOCKS):
+            flipped = psum.tile([P, P], BF16, name=f"flipped{i}")
+            nc.tensor.transpose(flipped[:], node_rows[i][:], identity[:])
+            if i % 2 == 0:
+                nc.vector.tensor_copy(node_columns[:, i * P : (i + 1) * P], flipped[:])
+            else:
+                nc.scalar.copy(node_columns[:, i * P : (i + 1) * P], flipped[:])
+
+        for j in range(OUT_BLOCKS):
+            edge_sum = psum.tile([P, EDGES], F32, name=f"edge_sum{j}")
+            for t in range(ENDS):
+                nc.tensor.matmul(
+                    edge_sum[:],
+                    weights[:, t, j * P : (j + 1) * P],
+                    node_columns[:].indirect(offsets[:, t * COLS_PER_END : (t + 1) * COLS_PER_END]),
+                    start=(t == 0),
+                    stop=(t == ENDS - 1),
+                )
+            result = held.tile([P, EDGES], F32, name=f"result{j}")
+            if j % 2 == 0:
+                nc.scalar.activation(
+                    result[:], edge_sum[:], mybir.ActivationFunctionType.Relu, bias=bias[:, j : j + 1]
+                )
+                nc.scalar.dma_start(out[j * P : (j + 1) * P, :], result[:])
+            else:
+                nc.vector.tensor_scalar(
+                    result[:],
+                    edge_sum[:],
+                    bias[:, j : j + 1],
+                    0.0,
+                    op0=mybir.AluOpType.add,
+                    op1=mybir.AluOpType.max,
+                )
+                nc.sync.dma_start(out[j * P : (j + 1) * P, :], result[:])

@@ -11,6 +11,8 @@ OUT_FEATURES = 256
 NODE_BLOCKS = NODES // P
 OUT_BLOCKS = OUT_FEATURES // P
 COLS_PER_END = EDGES // 16
+BANK = 512
+WARM_UPS = 4
 
 FLOPS = 2 * ENDS * P * OUT_FEATURES * EDGES
 
@@ -34,6 +36,12 @@ def tile_gather_matmul_kernel(tc, table, w, b, offs, out):
         bias = held.tile([P, OUT_BLOCKS], F32, name="bias")
         with nc.allow_non_contiguous_dma(reason="256 single float32 values, one to a partition and column"):
             nc.scalar.dma_start(bias[:], b.rearrange("(j p) o -> p (j o)", p=P))
+
+        zeros = held.tile([P, BANK], BF16, name="zeros")
+        nc.vector.memset(zeros[:], 0.0)
+        unread = psum.tile([P, BANK], F32, name="unread")
+        for warm_up in range(WARM_UPS):
+            nc.tensor.matmul(unread[:], zeros[:, 0:P], zeros[:], start=True, stop=True)
 
         identity = held.tile([P, P], BF16, name="identity")
         make_identity(nc, identity[:])

@@ -12,7 +12,7 @@ NODE_BLOCKS = NODES // P
 OUT_BLOCKS = OUT_FEATURES // P
 COLS_PER_END = EDGES // 16
 BANK = 512
-WARM_UPS = 4
+WARM_UPS = 3
 
 FLOPS = 2 * ENDS * P * OUT_FEATURES * EDGES
 
@@ -23,6 +23,14 @@ def tile_gather_matmul_kernel(tc, table, w, b, offs, out):
         tc.tile_pool(name="held", bufs=1) as held,
         tc.psum_pool(name="psum", bufs=1) as psum,
     ):
+        zeros = held.tile([P, P], BF16, name="zeros")
+        nc.vector.memset(zeros[:], 0.0)
+        unread = psum.tile([P, BANK // P, P], F32, name="unread")
+        for warm_up in range(WARM_UPS):
+            nc.tensor.matmul(
+                unread[:], zeros[:], zeros[:].unsqueeze(1).to_broadcast([P, BANK // P, P]), start=True, stop=True
+            )
+
         offsets = held.tile([P, ENDS * COLS_PER_END], U16, name="offsets")
         nc.sync.dma_start(offsets[:], offs)
 
@@ -36,12 +44,6 @@ def tile_gather_matmul_kernel(tc, table, w, b, offs, out):
         bias = held.tile([P, OUT_BLOCKS], F32, name="bias")
         with nc.allow_non_contiguous_dma(reason="256 single float32 values, one to a partition and column"):
             nc.scalar.dma_start(bias[:], b.rearrange("(j p) o -> p (j o)", p=P))
-
-        zeros = held.tile([P, BANK], BF16, name="zeros")
-        nc.vector.memset(zeros[:], 0.0)
-        unread = psum.tile([P, BANK], F32, name="unread")
-        for warm_up in range(WARM_UPS):
-            nc.tensor.matmul(unread[:], zeros[:, 0:P], zeros[:], start=True, stop=True)
 
         identity = held.tile([P, P], BF16, name="identity")
         make_identity(nc, identity[:])

@@ -11,8 +11,6 @@ OUT_FEATURES = 256
 NODE_BLOCKS = NODES // P
 OUT_BLOCKS = OUT_FEATURES // P
 COLS_PER_END = EDGES // 16
-BANK = 512
-WARM_UPS = 3
 
 FLOPS = 2 * ENDS * P * OUT_FEATURES * EDGES
 
@@ -23,21 +21,13 @@ def tile_gather_matmul_kernel(tc, table, w, b, offs, out):
         tc.tile_pool(name="held", bufs=1) as held,
         tc.psum_pool(name="psum", bufs=1) as psum,
     ):
-        zeros = held.tile([P, P], BF16, name="zeros")
-        nc.vector.memset(zeros[:], 0.0)
-        unread = psum.tile([P, BANK // P, P], F32, name="unread")
-        for warm_up in range(WARM_UPS):
-            nc.tensor.matmul(
-                unread[:], zeros[:], zeros[:].unsqueeze(1).to_broadcast([P, BANK // P, P]), start=True, stop=True
-            )
-
-        offsets = held.tile([P, ENDS * COLS_PER_END], U16, name="offsets")
-        nc.sync.dma_start(offsets[:], offs)
-
         node_rows = [held.tile([P, P], BF16, name=f"node_rows{i}") for i in range(NODE_BLOCKS)]
         for i in range(NODE_BLOCKS):
             queue = nc.sync if i % 2 == 0 else nc.scalar
             queue.dma_start(node_rows[i][:], table[i * P : (i + 1) * P, :])
+
+        offsets = held.tile([P, ENDS * COLS_PER_END], U16, name="offsets")
+        nc.sync.dma_start(offsets[:], offs)
 
         weights = held.tile([P, ENDS, OUT_FEATURES], BF16, name="weights")
         nc.sync.dma_start(weights[:], w.rearrange("t k m -> k t m"))
@@ -52,10 +42,7 @@ def tile_gather_matmul_kernel(tc, table, w, b, offs, out):
         for i in range(NODE_BLOCKS):
             flipped = psum.tile([P, P], BF16, name=f"flipped{i}")
             nc.tensor.transpose(flipped[:], node_rows[i][:], identity[:])
-            if i % 2 == 0:
-                nc.vector.tensor_copy(node_columns[:, i * P : (i + 1) * P], flipped[:])
-            else:
-                nc.scalar.copy(node_columns[:, i * P : (i + 1) * P], flipped[:])
+            nc.vector.tensor_copy(node_columns[:, i * P : (i + 1) * P], flipped[:])
 
         for j in range(OUT_BLOCKS):
             edge_sum = psum.tile([P, EDGES], F32, name=f"edge_sum{j}")
@@ -68,18 +55,13 @@ def tile_gather_matmul_kernel(tc, table, w, b, offs, out):
                     stop=(t == ENDS - 1),
                 )
             result = held.tile([P, EDGES], F32, name=f"result{j}")
-            if j % 2 == 0:
-                nc.scalar.activation(
-                    result[:], edge_sum[:], mybir.ActivationFunctionType.Relu, bias=bias[:, j : j + 1]
-                )
-                nc.scalar.dma_start(out[j * P : (j + 1) * P, :], result[:])
-            else:
-                nc.vector.tensor_scalar(
-                    result[:],
-                    edge_sum[:],
-                    bias[:, j : j + 1],
-                    0.0,
-                    op0=mybir.AluOpType.add,
-                    op1=mybir.AluOpType.max,
-                )
-                nc.sync.dma_start(out[j * P : (j + 1) * P, :], result[:])
+            nc.vector.tensor_scalar(
+                result[:],
+                edge_sum[:],
+                bias[:, j : j + 1],
+                0.0,
+                op0=mybir.AluOpType.add,
+                op1=mybir.AluOpType.max,
+            )
+            queue = nc.sync if j % 2 == 0 else nc.scalar
+            queue.dma_start(out[j * P : (j + 1) * P, :], result[:])

@@ -42,7 +42,10 @@ def tile_gather_matmul_kernel(tc, table, w, b, offs, out):
         for i in range(NODE_BLOCKS):
             flipped = psum.tile([P, P], BF16, name=f"flipped{i}")
             nc.tensor.transpose(flipped[:], node_rows[i][:], identity[:])
-            nc.vector.tensor_copy(node_columns[:, i * P : (i + 1) * P], flipped[:])
+            if i % 2 == 0:
+                nc.scalar.copy(node_columns[:, i * P : (i + 1) * P], flipped[:])
+            else:
+                nc.vector.tensor_copy(node_columns[:, i * P : (i + 1) * P], flipped[:])
 
         for j in range(OUT_BLOCKS):
             edge_sum = psum.tile([P, EDGES], F32, name=f"edge_sum{j}")
@@ -55,13 +58,18 @@ def tile_gather_matmul_kernel(tc, table, w, b, offs, out):
                     stop=(t == ENDS - 1),
                 )
             result = held.tile([P, EDGES], F32, name=f"result{j}")
-            nc.vector.tensor_scalar(
-                result[:],
-                edge_sum[:],
-                bias[:, j : j + 1],
-                0.0,
-                op0=mybir.AluOpType.add,
-                op1=mybir.AluOpType.max,
-            )
-            queue = nc.sync if j % 2 == 0 else nc.scalar
-            queue.dma_start(out[j * P : (j + 1) * P, :], result[:])
+            if j % 2 == 0:
+                nc.scalar.activation(
+                    result[:], edge_sum[:], mybir.ActivationFunctionType.Relu, bias=bias[:, j : j + 1]
+                )
+                nc.scalar.dma_start(out[j * P : (j + 1) * P, :], result[:])
+            else:
+                nc.vector.tensor_scalar(
+                    result[:],
+                    edge_sum[:],
+                    bias[:, j : j + 1],
+                    0.0,
+                    op0=mybir.AluOpType.add,
+                    op1=mybir.AluOpType.max,
+                )
+                nc.sync.dma_start(out[j * P : (j + 1) * P, :], result[:])

@@ -42,10 +42,7 @@ def tile_gather_matmul_kernel(tc, table, w, b, offs, out):
         for i in range(NODE_BLOCKS):
             flipped = psum.tile([P, P], BF16, name=f"flipped{i}")
             nc.tensor.transpose(flipped[:], node_rows[i][:], identity[:])
-            if i % 2 == 0:
-                nc.scalar.copy(node_columns[:, i * P : (i + 1) * P], flipped[:])
-            else:
-                nc.vector.tensor_copy(node_columns[:, i * P : (i + 1) * P], flipped[:])
+            nc.vector.tensor_copy(node_columns[:, i * P : (i + 1) * P], flipped[:])
 
         for j in range(OUT_BLOCKS):
             edge_sum = psum.tile([P, EDGES], F32, name=f"edge_sum{j}")

@@ -38,6 +38,9 @@ def tile_gather_matmul_kernel(tc, table, w, b, offs, out):
         identity = held.tile([P, P], BF16, name="identity")
         make_identity(nc, identity[:])
 
+        warmed = held.tile([P, 1], F32, name="warmed")
+        nc.scalar.activation(warmed[:], identity[:, 0:1], mybir.ActivationFunctionType.Relu)
+
         node_columns = held.tile([P, NODES], BF16, name="node_columns")
         for i in range(NODE_BLOCKS):
             flipped = psum.tile([P, P], BF16, name=f"flipped{i}")

@@ -32,8 +32,8 @@ def tile_gather_matmul_kernel(tc, table, w, b, offs, out):
         weights = held.tile([P, ENDS, OUT_FEATURES], BF16, name="weights")
         nc.sync.dma_start(weights[:], w.rearrange("t k m -> k t m"))
         bias = held.tile([P, OUT_BLOCKS], F32, name="bias")
-        with nc.allow_non_contiguous_dma(reason="256 single float32 values, one to a partition and column"):
-            nc.scalar.dma_start(bias[:], b.rearrange("(j p) o -> p (j o)", p=P))
+        nc.scalar.dma_start(bias[:], b.rearrange("(p j) o -> p (j o)", j=OUT_BLOCKS))
+        out_rows = out.rearrange("(p j) v -> p j v", j=OUT_BLOCKS)
 
         identity = held.tile([P, P], BF16, name="identity")
         make_identity(nc, identity[:])
@@ -52,7 +52,7 @@ def tile_gather_matmul_kernel(tc, table, w, b, offs, out):
             for t in range(ENDS):
                 nc.tensor.matmul(
                     edge_sum[:],
-                    weights[:, t, j * P : (j + 1) * P],
+                    weights[:, t, j::OUT_BLOCKS],
                     node_columns[:].indirect(offsets[:, t * COLS_PER_END : (t + 1) * COLS_PER_END]),
                     start=(t == 0),
                     stop=(t == ENDS - 1),
@@ -62,7 +62,7 @@ def tile_gather_matmul_kernel(tc, table, w, b, offs, out):
                 nc.scalar.activation(
                     result[:], edge_sum[:], mybir.ActivationFunctionType.Relu, bias=bias[:, j : j + 1]
                 )
-                nc.scalar.dma_start(out[j * P : (j + 1) * P, :], result[:])
+                nc.scalar.dma_start(out_rows[:, j, :], result[:])
             else:
                 nc.vector.tensor_scalar(
                     result[:],
@@ -72,4 +72,4 @@ def tile_gather_matmul_kernel(tc, table, w, b, offs, out):
                     op0=mybir.AluOpType.add,
                     op1=mybir.AluOpType.max,
                 )
-                nc.sync.dma_start(out[j * P : (j + 1) * P, :], result[:])
+                nc.sync.dma_start(out_rows[:, j, :], result[:])

@@ -21,9 +21,12 @@ def tile_gather_matmul_kernel(tc, table, w, b, offs, out):
         tc.tile_pool(name="held", bufs=1) as held,
         tc.psum_pool(name="psum", bufs=1) as psum,
     ):
+        bias = held.tile([P, OUT_BLOCKS], F32, name="bias")
         node_rows = [held.tile([P, P], BF16, name=f"node_rows{i}") for i in range(NODE_BLOCKS)]
         for i in range(NODE_BLOCKS):
             queue = nc.sync if i % 2 == 0 else nc.scalar
+            if i == NODE_BLOCKS - 1:
+                queue.dma_start(bias[:], b.rearrange("(p j) o -> p (j o)", j=OUT_BLOCKS))
             queue.dma_start(node_rows[i][:], table[i * P : (i + 1) * P, :])
 
         offsets = held.tile([P, ENDS * COLS_PER_END], U16, name="offsets")
@@ -31,8 +34,6 @@ def tile_gather_matmul_kernel(tc, table, w, b, offs, out):
 
         weights = held.tile([P, ENDS, OUT_FEATURES], BF16, name="weights")
         nc.sync.dma_start(weights[:], w.rearrange("t k m -> k t m"))
-        bias = held.tile([P, OUT_BLOCKS], F32, name="bias")
-        nc.scalar.dma_start(bias[:], b.rearrange("(p j) o -> p (j o)", j=OUT_BLOCKS))
         out_rows = out.rearrange("(p j) v -> p j v", j=OUT_BLOCKS)
 
         identity = held.tile([P, P], BF16, name="identity")

import concourse.mybir as mybir
from concourse.masks import make_identity

BF16, F32, U16 = mybir.dt.bfloat16, mybir.dt.float32, mybir.dt.uint16

P = 128
NODES = 512
ENDS = 2
EDGES = 128
OUT_FEATURES = 256
NODE_BLOCKS = NODES // P
OUT_BLOCKS = OUT_FEATURES // P
COLS_PER_END = EDGES // 16

FLOPS = 2 * ENDS * P * OUT_FEATURES * EDGES


def tile_gather_matmul_kernel(tc, table, w, b, offs, out):
    nc = tc.nc
    with (
        tc.tile_pool(name="held", bufs=1) as held,
        tc.psum_pool(name="psum", bufs=1) as psum,
    ):
        bias = held.tile([P, OUT_BLOCKS], F32, name="bias")
        node_rows = [held.tile([P, P], BF16, name=f"node_rows{i}") for i in range(NODE_BLOCKS)]
        for i in range(NODE_BLOCKS):
            queue = nc.sync if i % 2 == 0 else nc.scalar
            if i == NODE_BLOCKS - 1:
                queue.dma_start(bias[:], b.rearrange("(p j) o -> p (j o)", j=OUT_BLOCKS))
            queue.dma_start(node_rows[i][:], table[i * P : (i + 1) * P, :])

        offsets = held.tile([P, ENDS * COLS_PER_END], U16, name="offsets")
        nc.sync.dma_start(offsets[:], offs)

        weights = held.tile([P, ENDS, OUT_FEATURES], BF16, name="weights")
        nc.sync.dma_start(weights[:], w.rearrange("t k m -> k t m"))
        out_rows = out.rearrange("(p j) v -> p j v", j=OUT_BLOCKS)

        identity = held.tile([P, P], BF16, name="identity")
        make_identity(nc, identity[:])

        warmed = held.tile([P, 1], F32, name="warmed")
        nc.scalar.activation(warmed[:], identity[:, 0:1], mybir.ActivationFunctionType.Relu)

        node_columns = held.tile([P, NODES], BF16, name="node_columns")
        for i in range(NODE_BLOCKS):
            flipped = psum.tile([P, P], BF16, name=f"flipped{i}")
            nc.tensor.transpose(flipped[:], node_rows[i][:], identity[:])
            nc.vector.tensor_copy(node_columns[:, i * P : (i + 1) * P], flipped[:])

        for j in range(OUT_BLOCKS):
            edge_sum = psum.tile([P, EDGES], F32, name=f"edge_sum{j}")
            for t in range(ENDS):
                nc.tensor.matmul(
                    edge_sum[:],
                    weights[:, t, j::OUT_BLOCKS],
                    node_columns[:].indirect(offsets[:, t * COLS_PER_END : (t + 1) * COLS_PER_END]),
                    start=(t == 0),
                    stop=(t == ENDS - 1),
                )
            result = held.tile([P, EDGES], F32, name=f"result{j}")
            if j % 2 == 0:
                nc.scalar.activation(
                    result[:], edge_sum[:], mybir.ActivationFunctionType.Relu, bias=bias[:, j : j + 1]
                )
                nc.scalar.dma_start(out_rows[:, j, :], result[:])
            else:
                nc.vector.tensor_scalar(
                    result[:],
                    edge_sum[:],
                    bias[:, j : j + 1],
                    0.0,
                    op0=mybir.AluOpType.add,
                    op1=mybir.AluOpType.max,
                )
                nc.sync.dma_start(out_rows[:, j, :], result[:])
